import numpy as np
import ml_dtypes


def mxq(x, axis, fmt="e4m3"):
    dtype, down = {"e4m3": (ml_dtypes.float8_e4m3fn, 7), "e5m2": (ml_dtypes.float8_e5m2, 14)}[fmt]
    v = np.moveaxis(np.asarray(x, np.float32).astype(ml_dtypes.bfloat16).astype(np.float64), axis, -1)
    blocks = v.reshape(v.shape[:-1] + (-1, 32))
    amax = np.abs(blocks).max(-1, keepdims=True)
    byte = np.maximum(np.where(amax > 0, np.frexp(amax)[1] - 1 + 127, 0) - down, 1)
    scale = np.exp2(byte - 127.0)
    codes = (blocks / scale).astype(np.float32).astype(dtype).astype(np.float64)
    return np.moveaxis((codes * scale).reshape(v.shape), -1, axis)


WIDE = False


def mx_kscale(k):
    if not WIDE:
        return np.ones(k)
    levels = np.array([30, -30])
    if k % 512:
        return np.exp2(np.random.permutation(np.resize(levels, k // 32))).repeat(32)
    a = np.empty((k // 512, 16))
    for p in range(k // 512):
        a[p, :8] = np.random.permutation(np.resize(levels, 8))
        for g in range(8):
            far = levels[np.abs(levels - a[p, g]) >= 10]
            a[p, g + 8] = far[np.random.randint(len(far))]
    return np.exp2(a.ravel()).repeat(32)


def f64(x):
    return np.asarray(x).astype(np.float64)


def striped(idx):
    return np.tile(np.asarray(idx).reshape(-1, 16).T, (8, 1)).astype(np.uint16)


def unstriped(offs):
    return offs[:16].T.reshape(-1).astype(np.int64)


def striped8(idx):
    return np.asarray(idx).reshape(8, -1, 16).transpose(0, 2, 1).reshape(128, -1).astype(np.uint16)


def unstriped8(offs):
    return offs.reshape(8, 16, -1).transpose(0, 2, 1).reshape(8, -1).astype(np.int64)


def pick8(x, idx, run):
    r = np.arange(len(x))
    return x[r[:, None], idx[r % (8 * run) // run]]


E2M1 = np.array([0.0, 0.5, 1.0, 1.5, 2.0, 3.0, 4.0, 6.0, -0.0, -0.5, -1.0, -1.5, -2.0, -3.0, -4.0, -6.0])


def pack_weight(w, fmt):
    k, n = w.shape
    w = f64(np.asarray(w, np.float32).astype(ml_dtypes.bfloat16)).reshape(k // 32, 32, n)
    amax = np.abs(w).max(1)
    if fmt in ("e4m3", "e5m2"):
        byte = np.frexp(amax)[1] - 1 + 127 - (7 if fmt == "e4m3" else 14)
    else:
        mant, ex = np.frexp(amax / 6.0)
        byte = np.where(mant > 0.5, ex, ex - 1) + 127
    byte = np.clip(np.where(amax > 0, byte, 1), 1, 254)
    scaled = (w * np.exp2(127.0 - byte)[:, None, :]).reshape(k, n).astype(np.float32)
    by_word = np.ascontiguousarray(scaled.reshape(k // 512, 128, 4, n).transpose(0, 1, 3, 2))
    if fmt in ("e4m3", "e5m2"):
        words = by_word.astype(ml_dtypes.float8_e4m3fn if fmt == "e4m3" else ml_dtypes.float8_e5m2).view(np.uint8)
    else:
        c = by_word.astype(ml_dtypes.float4_e2m1fn).view(np.uint8) & 0xF
        words = (c[..., 0::2] | (c[..., 1::2] << 4)).reshape(k // 512, 128, 2 * n)
    return np.ascontiguousarray(words), np.ascontiguousarray(byte.astype(np.uint8).reshape(k // 512, 16, n))


def unpack_weight(words, scales, fmt):
    g, _, n = scales.shape
    words = np.ascontiguousarray(words).reshape(g, 128, n, -1)
    if fmt in ("e4m3", "e5m2"):
        vals = words.view(ml_dtypes.float8_e4m3fn if fmt == "e4m3" else ml_dtypes.float8_e5m2).astype(np.float64)
    else:
        nib = np.empty((g, 128, n, 4), np.uint8)
        nib[..., 0::2] = words & 0xF
        nib[..., 1::2] = words >> 4
        vals = E2M1[nib]
    vals = vals * np.repeat(np.exp2(scales.astype(np.float64) - 127.0), 8, axis=1)[..., None]
    return vals.transpose(0, 1, 3, 2).reshape(g * 512, n)


K, T, Z, J, R, C, O, N = 512, 1024, 1024, 256, 512, 512, 128, 256


def setup_inputs():
    n = np.random.standard_normal
    idx = np.random.permutation(T)[:J]
    idx2 = np.random.permutation(Z)[:J]
    idx3 = np.stack([np.random.permutation(C)[:J] for _ in range(8)])
    idx4 = np.stack([np.random.permutation(C)[:O] for _ in range(8)])
    idx5 = np.random.permutation(J)[:O]
    fk = mx_kscale(K)
    fr = mx_kscale(R)
    xtp = pack_weight(n((K, T)) / fk[:, None], "e2m1")
    xop = pack_weight(n((K, Z)) / fk[:, None], "e4m3")
    wp = pack_weight(n((K, R)) * 1 / np.sqrt(K) * fk[:, None] * fr, "e4m3")
    w2p = pack_weight(n((K, R)) * 1 / np.sqrt(K) * fk[:, None] * fr, "e5m2")
    wbp = pack_weight(n((R, N)) * 1 / np.sqrt(R) / fr[:, None], "e2m1")
    return {
        "xt_words": xtp[0],
        "xt_scales": xtp[1],
        "xo_words": xop[0],
        "xo_scales": xop[1],
        "w_words": wp[0],
        "w_scales": wp[1],
        "w2_words": w2p[0],
        "w2_scales": w2p[1],
        "sa": (np.random.uniform(0.5, 1.6, (R, 1))).astype(np.float32),
        "wb_words": wbp[0],
        "wb_scales": wbp[1],
        "offs": striped(idx),
        "offs2": striped(idx2),
        "offs3": striped8(idx3),
        "offs4": striped8(idx4),
        "offs5": striped(idx5),
    }


def reference(xt_words, xt_scales, xo_words, xo_scales, w_words, w_scales, w2_words, w2_scales, sa, wb_words, wb_scales, offs, offs2, offs3, offs4, offs5):
    idx = unstriped(offs)
    idx2 = unstriped(offs2)
    idx3 = unstriped8(offs3)
    idx4 = unstriped8(offs4)
    idx5 = unstriped(offs5)
    xtu = unpack_weight(xt_words, xt_scales, "e2m1")
    xou = unpack_weight(xo_words, xo_scales, "e4m3")
    wu = unpack_weight(w_words, w_scales, "e4m3")
    w2u = unpack_weight(w2_words, w2_scales, "e5m2")
    wbu = unpack_weight(wb_words, wb_scales, "e2m1")
    xtidxg = xtu[:, idx]
    xoidx2g = xou[:, idx2]
    a = wu.T @ xtidxg + w2u.T @ xoidx2g
    b = w2u.T @ xtidxg + wu.T @ xoidx2g
    pw = np.zeros((R, C))
    pw[np.arange(R)[:, None], idx3[np.arange(R) % 512 // 64]] = a
    hid = np.abs(pick8(pw, idx4, 64) * f64(sa) - b[:, idx5])
    hidq = mxq(hid, 0, "e5m2")
    y = wbu.T @ hidq
    return y

@@ -1,0 +1,167 @@
+from contextlib import ExitStack
+
+import concourse.mybir as mybir
+
+F32 = mybir.dt.float32
+BF16 = mybir.dt.bfloat16
+I32 = mybir.dt.int32
+U32 = mybir.dt.uint32
+U16 = mybir.dt.uint16
+U8 = mybir.dt.uint8
+E4M3 = mybir.dt.float8_e4m3fn_x4
+E5M2 = mybir.dt.float8_e5m2_x4
+E2M1 = mybir.dt.float4_e2m1fn_x4
+ACT = mybir.ActivationFunctionType
+ALU = mybir.AluOpType
+
+P = 128
+PACK = 4
+K, T, Z, J, R, C, O, N = 512, 1024, 1024, 256, 512, 512, 128, 256
+
+FLOPS = 4 * 2 * K * R * J + 2 * R * N * O
+
+
+def load_scale_rows(queue, tile_cols, scales, first_partition):
+    rows = scales[0].bitcast(I32).rearrange("(h q r) c -> q r h c", h=2, q=2)
+    for q in range(2):
+        p0 = first_partition + 32 * q
+        queue.dma_start(
+            out=tile_cols[p0 : p0 + 4, :].bitcast(I32).rearrange("p (h c) -> p h c", h=2),
+            in_=rows[q],
+        )
+
+
+def tile_list_groupboard_crossed_one_plain_kernel(
+    tc, xt_words, xt_scales, xo_words, xo_scales, w_words, w_scales, w2_words, w2_scales,
+    sa, wb_words, wb_scales, offs, offs2, offs3, offs4, offs5, out,
+):
+    nc = tc.nc
+    with ExitStack() as ctx:
+        keep = ctx.enter_context(tc.tile_pool(name="keep", bufs=1))
+        psum = ctx.enter_context(tc.psum_pool(name="psum", bufs=1))
+
+        list1 = keep.tile([P, J // 16], U16, name="list1")
+        list2 = keep.tile([P, J // 16], U16, name="list2")
+        list3 = keep.tile([P, J // 16], U16, name="list3")
+        list4 = keep.tile([P, O // 16], U16, name="list4")
+        list5 = keep.tile([P, O // 16], U16, name="list5")
+
+        xt_w = keep.tile([P, T], U16, name="xt_w", align_bytes=64)
+        xo_w = keep.tile([P, Z], U32, name="xo_w", align_bytes=64)
+        xt_s = keep.tile([P, 2 * T], U8, name="xt_s", align_bytes=64)
+        xo_s = keep.tile([P, 2 * Z], U8, name="xo_s", align_bytes=64)
+        ws_raw = keep.tile([P, 4 * R], U8, name="ws_raw", align_bytes=64)
+        w_raw = keep.tile([P, R], U32, name="w_raw", align_bytes=64)
+        w2_raw = keep.tile([P, R], U32, name="w2_raw", align_bytes=64)
+        wb_w = keep.tile([P, 2 * N], U8, name="wb_w", align_bytes=64)
+        wb_s = keep.tile([P, N], U8, name="wb_s", align_bytes=64)
+        sa_t = keep.tile([P, PACK], F32, name="sa_t")
+        pages = [keep.tile([P, C], F32, name=f"page{t}") for t in range(PACK)]
+
+        nc.gpsimd.memset(xt_s[0:64, :].bitcast(I32), 0)
+        nc.vector.memset(ws_raw[:].bitcast(I32), 0)
+        nc.vector.memset(xo_s[64:128, :].bitcast(I32), 0)
+        for t in range(PACK):
+            nc.gpsimd.memset(pages[t][:], 0.0)
+        nc.gpsimd.memset(wb_s[:].bitcast(I32), 0)
+
+        load_scale_rows(nc.scalar, xt_s[:], xt_scales, 0)
+        load_scale_rows(nc.scalar, ws_raw[:, 2 * R : 4 * R], w_scales, 0)
+        load_scale_rows(nc.scalar, ws_raw[:, 0 : 2 * R], w2_scales, 64)
+        load_scale_rows(nc.scalar, xo_s[:], xo_scales, 64)
+
+        nc.sync.dma_start(out=xt_w[:].bitcast(I32), in_=xt_words[0].bitcast(I32))
+        nc.sync.dma_start(list1[:], offs)
+        nc.sync.dma_start(out=xo_w[:].bitcast(I32), in_=xo_words[0].rearrange("p n t -> p (n t)").bitcast(I32))
+        nc.sync.dma_start(list2[:], offs2)
+        nc.sync.dma_start(out=w_raw[:].bitcast(I32), in_=w_words[0].rearrange("p n t -> p (n t)").bitcast(I32))
+        nc.sync.dma_start(out=w2_raw[:].bitcast(I32), in_=w2_words[0].rearrange("p n t -> p (n t)").bitcast(I32))
+        nc.sync.dma_start(list3[:], offs3)
+        nc.sync.dma_start(list5[:], offs5)
+        nc.sync.dma_start(list4[:], offs4)
+
+        nc.gpsimd.dma_start(out=sa_t[:], in_=sa.rearrange("(p t) o -> p (t o)", t=PACK))
+        nc.gpsimd.dma_start(out=wb_w[:].bitcast(I32), in_=wb_words[0].bitcast(I32))
+        wb_rows = wb_scales[0].bitcast(I32)
+        for q in range(4):
+            nc.sync.dma_start(out=wb_s[32 * q : 32 * q + 4, :].bitcast(I32), in_=wb_rows[4 * q : 4 * q + 4, :])
+
+        xt_g = keep.tile([P, J], U16, name="xt_g", align_bytes=64)
+        xo_g = keep.tile([P, J], U32, name="xo_g", align_bytes=64)
+        xt_gs = keep.tile([P, J], U8, name="xt_gs", align_bytes=64)
+        xo_gs = keep.tile([P, J], U8, name="xo_gs", align_bytes=64)
+        ws = [keep.tile([P, 2, P], U8, name=f"ws{t}", align_bytes=64) for t in range(PACK)]
+        w_p = keep.tile([P, PACK, P], U32, name="w_p", align_bytes=64)
+        w2_p = [keep.tile([P, P], U32, name=f"w2_p{t}", align_bytes=64) for t in range(PACK)]
+
+        xt_sw = keep.tile([P, T], U8, name="xt_sw", align_bytes=64)
+        xo_sw = keep.tile([P, Z], U8, name="xo_sw", align_bytes=64)
+        nc.vector.tensor_copy(out=xt_sw[0:64, :].bitcast(I32), in_=xt_s[0:64, 0:T].bitcast(I32))
+        nc.vector.tensor_copy(out=xt_sw[64:128, :].bitcast(I32), in_=xt_s[0:64, T : 2 * T].bitcast(I32))
+        nc.vector.tensor_copy(out=ws_raw[64:128, 2 * R : 3 * R].bitcast(I32), in_=ws_raw[0:64, 3 * R : 4 * R].bitcast(I32))
+        nc.vector.tensor_copy(out=ws_raw[0:64, R : 2 * R].bitcast(I32), in_=ws_raw[64:128, 0:R].bitcast(I32))
+        nc.vector.tensor_copy(out=xo_sw[0:64, :].bitcast(I32), in_=xo_s[64:128, 0:Z].bitcast(I32))
+        nc.vector.tensor_copy(out=xo_sw[64:128, :].bitcast(I32), in_=xo_s[64:128, Z : 2 * Z].bitcast(I32))
+        nc.vector.tensor_copy(xt_g[:], xt_w[:].indirect(list1[:]))
+        nc.vector.tensor_copy(xt_gs[:], xt_sw[:].indirect(list1[:]))
+        ws_dealt = ws_raw[:, R : 3 * R].rearrange("p (a m t) -> p t a m", a=2, t=PACK)
+        nc.gpsimd.tensor_copy(out=ws[0][:], in_=ws_dealt[:, 0])
+        nc.vector.tensor_copy(xo_gs[:], xo_sw[:].indirect(list2[:]))
+        nc.vector.tensor_copy(xo_g[:], xo_w[:].indirect(list2[:]))
+        for t in range(1, PACK):
+            nc.gpsimd.tensor_copy(out=ws[t][:], in_=ws_dealt[:, t])
+
+        nc.scalar.copy(out=w_p[:].rearrange("p t m -> p m t"), in_=w_raw[:].rearrange("p (m t) -> p m t", t=PACK))
+        w2_dealt = w2_raw[:].rearrange("p (m t) -> p t m", t=PACK)
+        for t in range(PACK):
+            nc.scalar.copy(out=w2_p[t][:], in_=w2_dealt[:, t])
+
+        picked = keep.tile([P, PACK, O], F32, name="picked")
+        b_pick = keep.tile([P, PACK, O], F32, name="b_pick")
+        diff = keep.tile([P, PACK, O], F32, name="diff")
+        a_sb = [keep.tile([P, J], F32, name=f"a_sb{t}") for t in range(PACK)]
+        b_sb = [keep.tile([P, J], F32, name=f"b_sb{t}") for t in range(PACK)]
+
+        def crossed(acc, t, x_first, x_second):
+            nc.tensor.matmul_mx(acc[:], lhsT=w_p[:, t, :].bitcast(E4M3), lhsT_scale=ws[t][:, 1, :],
+                                rhs=x_first[0], rhs_scale=x_first[1], start=True, stop=False)
+            nc.tensor.matmul_mx(acc[:], lhsT=w2_p[t][:].bitcast(E5M2), lhsT_scale=ws[t][:, 0, :],
+                                rhs=x_second[0], rhs_scale=x_second[1], start=False, stop=True)
+
+        tokens = (xt_g[:].bitcast(E2M1), xt_gs[:])
+        notes = (xo_g[:].bitcast(E4M3), xo_gs[:])
+        for t in range(PACK):
+            a_ps = psum.tile([P, J], F32, name="a_ps", tag=f"a{t}")
+            crossed(a_ps, t, tokens, notes)
+            nc.scalar.copy(out=a_sb[t][:], in_=a_ps[:])
+            nc.vector.tensor_copy(pages[t][:].indirect(list3[:]), a_sb[t][:])
+        for t in range(PACK):
+            b_ps = psum.tile([P, J], F32, name="b_ps", tag=f"b{t}")
+            crossed(b_ps, t, notes, tokens)
+            nc.scalar.copy(out=b_sb[t][:], in_=b_ps[:])
+            nc.scalar.activation(b_pick[:, t, :], b_sb[t][:].indirect(list5[:]), ACT.Copy)
+        for t in range(PACK):
+            nc.scalar.activation(picked[:, t, :], pages[t][:].indirect(list4[:]), ACT.Copy, scale=sa_t[:, t : t + 1])
+
+        nc.vector.tensor_tensor(diff[:, 0:3, :], picked[:, 0:3, :], b_pick[:, 0:3, :], ALU.subtract)
+        nc.vector.tensor_tensor(diff[:, 3, :], picked[:, 3, :], b_pick[:, 3, :], ALU.subtract)
+        hid = keep.tile([P, O, PACK], BF16, name="hid", align_bytes=64)
+        for u in range(2):
+            nc.scalar.activation(hid[:, :, 2 * u : 2 * u + 2],
+                                 diff[:, 2 * u : 2 * u + 2, :].rearrange("p t o -> p o t"), ACT.Abs)
+        hid_w = keep.tile([P, O], U32, name="hid_w", align_bytes=64)
+        hid_s = keep.tile([P, O], U8, name="hid_s", align_bytes=64)
+        nc.vector.quantize_mx(out=hid_w[:].bitcast(E5M2), scales=hid_s[:], in_=hid[:].rearrange("p o t -> p (o t)"))
+
+        for h in range(2):
+            y_ps = psum.tile([P, O], F32, name="y_ps", tag=f"a{h}")
+            nc.tensor.matmul_mx(y_ps[:], lhsT=wb_w[:, 2 * P * h : 2 * P * (h + 1)].bitcast(E2M1),
+                                lhsT_scale=wb_s[:, P * h : P * (h + 1)],
+                                rhs=hid_w[:].bitcast(E5M2), rhs_scale=hid_s[:], start=True, stop=True)
+            y_sb = keep.tile([P, O], F32, name=f"y_sb{h}")
+            if h == 0:
+                nc.vector.tensor_copy(out=y_sb[:], in_=y_ps[:])
+                nc.sync.dma_start(out=out[0:P, :], in_=y_sb[:])
+            else:
+                nc.scalar.copy(out=y_sb[:], in_=y_ps[:])
+                nc.scalar.dma_start(out=out[P : 2 * P, :], in_=y_sb[:])

@@ -31,6 +31,12 @@ def load_scale_rows(queue, tile_cols, scales, first_partition):
         )
 
 
+def load_plane(queue, plane, scales):
+    rows = scales[0].bitcast(I32)
+    for q in range(4):
+        queue.dma_start(out=plane[32 * q : 32 * q + 4, :].bitcast(I32), in_=rows[4 * q : 4 * q + 4, :])
+
+
 def tile_list_groupboard_crossed_one_plain_kernel(
     tc, xt_words, xt_scales, xo_words, xo_scales, w_words, w_scales, w2_words, w2_scales,
     sa, wb_words, wb_scales, offs, offs2, offs3, offs4, offs5, out,
@@ -49,8 +55,9 @@ def tile_list_groupboard_crossed_one_plain_kernel(
         xt_w = keep.tile([P, T], U16, name="xt_w", align_bytes=64)
         xo_w = keep.tile([P, Z], U32, name="xo_w", align_bytes=64)
         xt_s = keep.tile([P, 2 * T], U8, name="xt_s", align_bytes=64)
-        xo_s = keep.tile([P, 2 * Z], U8, name="xo_s", align_bytes=64)
-        ws_raw = keep.tile([P, 4 * R], U8, name="ws_raw", align_bytes=64)
+        xo_s = keep.tile([P, Z], U8, name="xo_s", align_bytes=64)
+        ws_raw = keep.tile([4, 8 * R], U8, name="ws_raw", align_bytes=64)
+        ws_pl = keep.tile([P, 2 * R], U8, name="ws_pl", align_bytes=64)
         w_raw = keep.tile([P, R], U32, name="w_raw", align_bytes=64)
         w2_raw = keep.tile([P, R], U32, name="w2_raw", align_bytes=64)
         wb_w = keep.tile([P, 2 * N], U8, name="wb_w", align_bytes=64)
@@ -58,33 +65,31 @@ def tile_list_groupboard_crossed_one_plain_kernel(
         sa_t = keep.tile([P, PACK], F32, name="sa_t")
         pages = [keep.tile([P, C], F32, name=f"page{t}") for t in range(PACK)]
 
-        nc.gpsimd.memset(xt_s[0:64, :].bitcast(I32), 0)
-        nc.vector.memset(ws_raw[:].bitcast(I32), 0)
-        nc.vector.memset(xo_s[64:128, :].bitcast(I32), 0)
+        nc.vector.memset(xt_s[64:128, :].bitcast(I32), 0)
+        nc.vector.memset(xo_s[:].bitcast(I32), 0)
+        nc.vector.memset(wb_s[:].bitcast(I32), 0)
+        nc.vector.memset(ws_pl[:].bitcast(I32), 0)
         for t in range(PACK):
             nc.gpsimd.memset(pages[t][:], 0.0)
-        nc.gpsimd.memset(wb_s[:].bitcast(I32), 0)
 
-        load_scale_rows(nc.scalar, xt_s[:], xt_scales, 0)
-        load_scale_rows(nc.scalar, ws_raw[:, 2 * R : 4 * R], w_scales, 0)
-        load_scale_rows(nc.scalar, ws_raw[:, 0 : 2 * R], w2_scales, 64)
-        load_scale_rows(nc.scalar, xo_s[:], xo_scales, 64)
-
+        load_scale_rows(nc.sync, xt_s[:], xt_scales, 64)
         nc.sync.dma_start(out=xt_w[:].bitcast(I32), in_=xt_words[0].bitcast(I32))
         nc.sync.dma_start(list1[:], offs)
+        ws_blocks = ws_raw[:].bitcast(I32).rearrange("p (q a c) -> p a q c", q=4, a=2)
+        for a, scales in enumerate((w2_scales, w_scales)):
+            nc.sync.dma_start(out=ws_blocks[:, a], in_=scales[0].bitcast(I32).rearrange("(q r) c -> r q c", q=4))
         nc.sync.dma_start(out=xo_w[:].bitcast(I32), in_=xo_words[0].rearrange("p n t -> p (n t)").bitcast(I32))
-        nc.sync.dma_start(list2[:], offs2)
         nc.sync.dma_start(out=w_raw[:].bitcast(I32), in_=w_words[0].rearrange("p n t -> p (n t)").bitcast(I32))
+        nc.sync.dma_start(list2[:], offs2)
         nc.sync.dma_start(out=w2_raw[:].bitcast(I32), in_=w2_words[0].rearrange("p n t -> p (n t)").bitcast(I32))
+        load_plane(nc.sync, xo_s, xo_scales)
         nc.sync.dma_start(list3[:], offs3)
         nc.sync.dma_start(list5[:], offs5)
         nc.sync.dma_start(list4[:], offs4)
 
-        nc.gpsimd.dma_start(out=sa_t[:], in_=sa.rearrange("(p t) o -> p (t o)", t=PACK))
-        nc.gpsimd.dma_start(out=wb_w[:].bitcast(I32), in_=wb_words[0].bitcast(I32))
-        wb_rows = wb_scales[0].bitcast(I32)
-        for q in range(4):
-            nc.sync.dma_start(out=wb_s[32 * q : 32 * q + 4, :].bitcast(I32), in_=wb_rows[4 * q : 4 * q + 4, :])
+        nc.sync.dma_start(out=sa_t[:], in_=sa.rearrange("(p t) o -> p (t o)", t=PACK))
+        nc.sync.dma_start(out=wb_w[:].bitcast(I32), in_=wb_words[0].bitcast(I32))
+        load_plane(nc.sync, wb_s, wb_scales)
 
         xt_g = keep.tile([P, J], U16, name="xt_g", align_bytes=64)
         xo_g = keep.tile([P, J], U32, name="xo_g", align_bytes=64)
@@ -95,19 +100,20 @@ def tile_list_groupboard_crossed_one_plain_kernel(
         w2_p = [keep.tile([P, P], U32, name=f"w2_p{t}", align_bytes=64) for t in range(PACK)]
 
         xt_sw = keep.tile([P, T], U8, name="xt_sw", align_bytes=64)
-        xo_sw = keep.tile([P, Z], U8, name="xo_sw", align_bytes=64)
-        nc.vector.tensor_copy(out=xt_sw[0:64, :].bitcast(I32), in_=xt_s[0:64, 0:T].bitcast(I32))
-        nc.vector.tensor_copy(out=xt_sw[64:128, :].bitcast(I32), in_=xt_s[0:64, T : 2 * T].bitcast(I32))
-        nc.vector.tensor_copy(out=ws_raw[64:128, 2 * R : 3 * R].bitcast(I32), in_=ws_raw[0:64, 3 * R : 4 * R].bitcast(I32))
-        nc.vector.tensor_copy(out=ws_raw[0:64, R : 2 * R].bitcast(I32), in_=ws_raw[64:128, 0:R].bitcast(I32))
-        nc.vector.tensor_copy(out=xo_sw[0:64, :].bitcast(I32), in_=xo_s[64:128, 0:Z].bitcast(I32))
-        nc.vector.tensor_copy(out=xo_sw[64:128, :].bitcast(I32), in_=xo_s[64:128, Z : 2 * Z].bitcast(I32))
-        nc.vector.tensor_copy(xt_g[:], xt_w[:].indirect(list1[:]))
-        nc.vector.tensor_copy(xt_gs[:], xt_sw[:].indirect(list1[:]))
-        ws_dealt = ws_raw[:, R : 3 * R].rearrange("p (a m t) -> p t a m", a=2, t=PACK)
+        nc.vector.tensor_copy(out=xt_sw[64:128, :].bitcast(I32), in_=xt_s[64:128, T : 2 * T].bitcast(I32))
+        nc.vector.tensor_copy(out=xt_sw[0:64, :].bitcast(I32), in_=xt_s[64:128, 0:T].bitcast(I32))
+        for q in range(4):
+            nc.vector.tensor_copy(out=ws_pl[32 * q : 32 * q + 4, :].bitcast(I32),
+                                  in_=ws_raw[0:4, 2 * R * q : 2 * R * (q + 1)].bitcast(I32))
+        H = J // 2
+        for u in range(2):
+            cols, lcols = slice(H * u, H * (u + 1)), slice(H // 16 * u, H // 16 * (u + 1))
+            nc.vector.tensor_copy(xt_gs[:, cols], xt_sw[:].indirect(list1[:, lcols]))
+            nc.vector.tensor_copy(xt_g[:, cols], xt_w[:].indirect(list1[:, lcols]))
+            nc.vector.tensor_copy(xo_g[:, cols], xo_w[:].indirect(list2[:, lcols]))
+            nc.vector.tensor_copy(xo_gs[:, cols], xo_s[:].indirect(list2[:, lcols]))
+        ws_dealt = ws_pl[:].rearrange("p (a m t) -> p t a m", a=2, t=PACK)
         nc.gpsimd.tensor_copy(out=ws[0][:], in_=ws_dealt[:, 0])
-        nc.vector.tensor_copy(xo_gs[:], xo_sw[:].indirect(list2[:]))
-        nc.vector.tensor_copy(xo_g[:], xo_w[:].indirect(list2[:]))
         for t in range(1, PACK):
             nc.gpsimd.tensor_copy(out=ws[t][:], in_=ws_dealt[:, t])
 
@@ -116,35 +122,48 @@ def tile_list_groupboard_crossed_one_plain_kernel(
         for t in range(PACK):
             nc.scalar.copy(out=w2_p[t][:], in_=w2_dealt[:, t])
 
-        picked = keep.tile([P, PACK, O], F32, name="picked")
         b_pick = keep.tile([P, PACK, O], F32, name="b_pick")
         diff = keep.tile([P, PACK, O], F32, name="diff")
         a_sb = [keep.tile([P, J], F32, name=f"a_sb{t}") for t in range(PACK)]
-        b_sb = [keep.tile([P, J], F32, name=f"b_sb{t}") for t in range(PACK)]
+        b_sb = [keep.tile([P, J], F32, name=f"b_sb{t}", tag=f"b_sb{t}") for t in range(PACK)]
 
-        def crossed(acc, t, x_first, x_second):
-            nc.tensor.matmul_mx(acc[:], lhsT=w_p[:, t, :].bitcast(E4M3), lhsT_scale=ws[t][:, 1, :],
-                                rhs=x_first[0], rhs_scale=x_first[1], start=True, stop=False)
-            nc.tensor.matmul_mx(acc[:], lhsT=w2_p[t][:].bitcast(E5M2), lhsT_scale=ws[t][:, 0, :],
-                                rhs=x_second[0], rhs_scale=x_second[1], start=False, stop=True)
+        def product(acc, first, second):
+            for n, (lhs, rhs) in enumerate((first, second)):
+                nc.tensor.matmul_mx(acc, lhsT=lhs[0], lhsT_scale=lhs[1], rhs=rhs[0], rhs_scale=rhs[1],
+                                    start=(n == 0), stop=(n == 1))
 
-        tokens = (xt_g[:].bitcast(E2M1), xt_gs[:])
-        notes = (xo_g[:].bitcast(E4M3), xo_gs[:])
-        for t in range(PACK):
+        def tokens(cols):
+            return xt_g[:, cols].bitcast(E2M1), xt_gs[:, cols]
+
+        def notes(cols):
+            return xo_g[:, cols].bitcast(E4M3), xo_gs[:, cols]
+
+        first = [(w_p[:, t, :].bitcast(E4M3), ws[t][:, 1, :]) for t in range(PACK)]
+        second = [(w2_p[t][:].bitcast(E5M2), ws[t][:, 0, :]) for t in range(PACK)]
+        whole = slice(0, J)
+        for u in range(2):
+            cols, lcols = slice(H * u, H * (u + 1)), slice(H // 16 * u, H // 16 * (u + 1))
+            a_half = psum.tile([P, H], F32, name="a_half", tag=("a0", "b3")[u])
+            product(a_half[:], (first[0], tokens(cols)), (second[0], notes(cols)))
+            nc.scalar.copy(out=a_sb[0][:, cols], in_=a_half[:])
+            nc.vector.tensor_copy(pages[0][:].indirect(list3[:, lcols]), a_sb[0][:, cols])
+        for t in range(1, PACK):
             a_ps = psum.tile([P, J], F32, name="a_ps", tag=f"a{t}")
-            crossed(a_ps, t, tokens, notes)
+            product(a_ps[:], (second[t], notes(whole)), (first[t], tokens(whole)))
             nc.scalar.copy(out=a_sb[t][:], in_=a_ps[:])
             nc.vector.tensor_copy(pages[t][:].indirect(list3[:]), a_sb[t][:])
         for t in range(PACK):
             b_ps = psum.tile([P, J], F32, name="b_ps", tag=f"b{t}")
-            crossed(b_ps, t, notes, tokens)
+            product(b_ps[:], (first[t], notes(whole)), (second[t], tokens(whole)))
             nc.scalar.copy(out=b_sb[t][:], in_=b_ps[:])
             nc.scalar.activation(b_pick[:, t, :], b_sb[t][:].indirect(list5[:]), ACT.Copy)
+        picked = [keep.tile([P, 2, O], F32, name=f"picked{u}", tag=f"b_sb{2 + u}") for u in range(2)]
         for t in range(PACK):
-            nc.scalar.activation(picked[:, t, :], pages[t][:].indirect(list4[:]), ACT.Copy, scale=sa_t[:, t : t + 1])
+            nc.scalar.activation(picked[t // 2][:, t % 2, :], pages[t][:].indirect(list4[:]), ACT.Copy, scale=sa_t[:, t : t + 1])
 
-        nc.vector.tensor_tensor(diff[:, 0:3, :], picked[:, 0:3, :], b_pick[:, 0:3, :], ALU.subtract)
-        nc.vector.tensor_tensor(diff[:, 3, :], picked[:, 3, :], b_pick[:, 3, :], ALU.subtract)
+        nc.vector.tensor_tensor(diff[:, 0:2, :], picked[0][:], b_pick[:, 0:2, :], ALU.subtract)
+        for t in (2, 3):
+            nc.vector.tensor_tensor(diff[:, t, :], picked[1][:, t - 2, :], b_pick[:, t, :], ALU.subtract)
         hid = keep.tile([P, O, PACK], BF16, name="hid", align_bytes=64)
         for u in range(2):
             nc.scalar.activation(hid[:, :, 2 * u : 2 * u + 2],

@@ -70,7 +70,7 @@ def tile_list_groupboard_crossed_one_plain_kernel(
         nc.vector.memset(wb_s[:].bitcast(I32), 0)
         nc.vector.memset(ws_pl[:].bitcast(I32), 0)
         for t in range(PACK):
-            nc.gpsimd.memset(pages[t][:], 0.0)
+            nc.vector.memset(pages[t][:], 0.0)
 
         load_scale_rows(nc.sync, xt_s[:], xt_scales, 64)
         nc.sync.dma_start(out=xt_w[:].bitcast(I32), in_=xt_words[0].bitcast(I32))
@@ -105,6 +105,8 @@ def tile_list_groupboard_crossed_one_plain_kernel(
         for q in range(4):
             nc.vector.tensor_copy(out=ws_pl[32 * q : 32 * q + 4, :].bitcast(I32),
                                   in_=ws_raw[0:4, 2 * R * q : 2 * R * (q + 1)].bitcast(I32))
+        ws_dealt = ws_pl[:].rearrange("p (a m t) -> p t a m", a=2, t=PACK)
+        nc.vector.tensor_copy(out=ws[0][:], in_=ws_dealt[:, 0])
         H = J // 2
         for u in range(2):
             cols, lcols = slice(H * u, H * (u + 1)), slice(H // 16 * u, H // 16 * (u + 1))
@@ -112,10 +114,8 @@ def tile_list_groupboard_crossed_one_plain_kernel(
             nc.vector.tensor_copy(xt_g[:, cols], xt_w[:].indirect(list1[:, lcols]))
             nc.vector.tensor_copy(xo_g[:, cols], xo_w[:].indirect(list2[:, lcols]))
             nc.vector.tensor_copy(xo_gs[:, cols], xo_s[:].indirect(list2[:, lcols]))
-        ws_dealt = ws_pl[:].rearrange("p (a m t) -> p t a m", a=2, t=PACK)
-        nc.gpsimd.tensor_copy(out=ws[0][:], in_=ws_dealt[:, 0])
         for t in range(1, PACK):
-            nc.gpsimd.tensor_copy(out=ws[t][:], in_=ws_dealt[:, t])
+            nc.vector.tensor_copy(out=ws[t][:], in_=ws_dealt[:, t])
 
         nc.scalar.copy(out=w_p[:].rearrange("p t m -> p m t"), in_=w_raw[:].rearrange("p (m t) -> p m t", t=PACK))
         w2_dealt = w2_raw[:].rearrange("p (m t) -> p t m", t=PACK)

@@ -21,20 +21,10 @@ K, T, Z, J, R, C, O, N = 512, 1024, 1024, 256, 512, 512, 128, 256
 FLOPS = 4 * 2 * K * R * J + 2 * R * N * O
 
 
-def load_scale_rows(queue, tile_cols, scales, first_partition):
-    rows = scales[0].bitcast(I32).rearrange("(h q r) c -> q r h c", h=2, q=2)
-    for q in range(2):
-        p0 = first_partition + 32 * q
-        queue.dma_start(
-            out=tile_cols[p0 : p0 + 4, :].bitcast(I32).rearrange("p (h c) -> p h c", h=2),
-            in_=rows[q],
-        )
-
-
 def load_plane(queue, plane, scales):
     rows = scales[0].bitcast(I32)
-    for q in range(4):
-        queue.dma_start(out=plane[32 * q : 32 * q + 4, :].bitcast(I32), in_=rows[4 * q : 4 * q + 4, :])
+    for r in range(4):
+        queue.dma_start(out=plane[r:P:32, :].bitcast(I32), in_=rows[r:16:4, :])
 
 
 def tile_list_groupboard_crossed_one_plain_kernel(
@@ -72,11 +62,13 @@ def tile_list_groupboard_crossed_one_plain_kernel(
         for t in range(PACK):
             nc.vector.memset(pages[t][:], 0.0)
 
-        load_scale_rows(nc.sync, xt_s[:], xt_scales, 64)
         nc.sync.dma_start(out=xt_w[:].bitcast(I32), in_=xt_words[0].bitcast(I32))
         nc.sync.dma_start(list1[:], offs)
         ws_blocks = ws_raw[:].bitcast(I32).rearrange("p (q a c) -> p a q c", q=4, a=2)
+        xt_rows = xt_scales[0].bitcast(I32).rearrange("(h q r) c -> q r h c", h=2, q=2)
         for a, scales in enumerate((w2_scales, w_scales)):
+            p0 = 64 + 32 * a
+            nc.sync.dma_start(out=xt_s[p0 : p0 + 4, :].bitcast(I32).rearrange("p (h c) -> p h c", h=2), in_=xt_rows[a])
             nc.sync.dma_start(out=ws_blocks[:, a], in_=scales[0].bitcast(I32).rearrange("(q r) c -> r q c", q=4))
         nc.sync.dma_start(out=xo_w[:].bitcast(I32), in_=xo_words[0].rearrange("p n t -> p (n t)").bitcast(I32))
         nc.sync.dma_start(out=w_raw[:].bitcast(I32), in_=w_words[0].rearrange("p n t -> p (n t)").bitcast(I32))
@@ -115,7 +107,7 @@ def tile_list_groupboard_crossed_one_plain_kernel(
             nc.vector.tensor_copy(xo_g[:, cols], xo_w[:].indirect(list2[:, lcols]))
             nc.vector.tensor_copy(xo_gs[:, cols], xo_s[:].indirect(list2[:, lcols]))
         for t in range(1, PACK):
-            nc.vector.tensor_copy(out=ws[t][:], in_=ws_dealt[:, t])
+            nc.gpsimd.tensor_copy(out=ws[t][:], in_=ws_dealt[:, t])
 
         nc.scalar.copy(out=w_p[:].rearrange("p t m -> p m t"), in_=w_raw[:].rearrange("p (m t) -> p m t", t=PACK))
         w2_dealt = w2_raw[:].rearrange("p (m t) -> p t m", t=PACK)

@@ -46,30 +46,30 @@ def tile_list_groupboard_crossed_one_plain_kernel(
         xo_w = keep.tile([P, Z], U32, name="xo_w", align_bytes=64)
         xt_s = keep.tile([P, 2 * T], U8, name="xt_s", align_bytes=64)
         xo_s = keep.tile([P, Z], U8, name="xo_s", align_bytes=64)
-        ws_raw = keep.tile([4, 8 * R], U8, name="ws_raw", align_bytes=64)
+        ws_raw = keep.tile([4, 8 * R], U8, name="ws_raw", tag="ws_raw", align_bytes=64)
         ws_pl = keep.tile([P, 2 * R], U8, name="ws_pl", align_bytes=64)
-        w_raw = keep.tile([P, R], U32, name="w_raw", align_bytes=64)
+        w_raw = keep.tile([P, R], U32, name="w_raw", tag="w_raw", align_bytes=64)
         w2_raw = keep.tile([P, R], U32, name="w2_raw", align_bytes=64)
         wb_w = keep.tile([P, 2 * N], U8, name="wb_w", align_bytes=64)
         wb_s = keep.tile([P, N], U8, name="wb_s", align_bytes=64)
         sa_t = keep.tile([P, PACK], F32, name="sa_t")
-        pages = [keep.tile([P, C], F32, name=f"page{t}") for t in range(PACK)]
+        pages = [keep.tile([P, C], F32, name=f"page{t}") for t in range(2)]
 
         nc.vector.memset(xt_s[64:128, :].bitcast(I32), 0)
         nc.vector.memset(xo_s[:].bitcast(I32), 0)
         nc.vector.memset(wb_s[:].bitcast(I32), 0)
         nc.vector.memset(ws_pl[:].bitcast(I32), 0)
-        for t in range(PACK):
+        for t in range(2):
             nc.vector.memset(pages[t][:], 0.0)
 
         nc.sync.dma_start(out=xt_w[:].bitcast(I32), in_=xt_words[0].bitcast(I32))
-        nc.sync.dma_start(list1[:], offs)
         ws_blocks = ws_raw[:].bitcast(I32).rearrange("p (q a c) -> p a q c", q=4, a=2)
         xt_rows = xt_scales[0].bitcast(I32).rearrange("(h q r) c -> q r h c", h=2, q=2)
         for a, scales in enumerate((w2_scales, w_scales)):
             p0 = 64 + 32 * a
-            nc.sync.dma_start(out=xt_s[p0 : p0 + 4, :].bitcast(I32).rearrange("p (h c) -> p h c", h=2), in_=xt_rows[a])
             nc.sync.dma_start(out=ws_blocks[:, a], in_=scales[0].bitcast(I32).rearrange("(q r) c -> r q c", q=4))
+            nc.sync.dma_start(out=xt_s[p0 : p0 + 4, :].bitcast(I32).rearrange("p (h c) -> p h c", h=2), in_=xt_rows[a])
+        nc.sync.dma_start(list1[:], offs)
         nc.sync.dma_start(out=xo_w[:].bitcast(I32), in_=xo_words[0].rearrange("p n t -> p (n t)").bitcast(I32))
         nc.sync.dma_start(out=w_raw[:].bitcast(I32), in_=w_words[0].rearrange("p n t -> p (n t)").bitcast(I32))
         nc.sync.dma_start(list2[:], offs2)
@@ -92,13 +92,13 @@ def tile_list_groupboard_crossed_one_plain_kernel(
         w2_p = [keep.tile([P, P], U32, name=f"w2_p{t}", align_bytes=64) for t in range(PACK)]
 
         xt_sw = keep.tile([P, T], U8, name="xt_sw", align_bytes=64)
-        nc.vector.tensor_copy(out=xt_sw[64:128, :].bitcast(I32), in_=xt_s[64:128, T : 2 * T].bitcast(I32))
-        nc.vector.tensor_copy(out=xt_sw[0:64, :].bitcast(I32), in_=xt_s[64:128, 0:T].bitcast(I32))
         for q in range(4):
             nc.vector.tensor_copy(out=ws_pl[32 * q : 32 * q + 4, :].bitcast(I32),
                                   in_=ws_raw[0:4, 2 * R * q : 2 * R * (q + 1)].bitcast(I32))
         ws_dealt = ws_pl[:].rearrange("p (a m t) -> p t a m", a=2, t=PACK)
         nc.vector.tensor_copy(out=ws[0][:], in_=ws_dealt[:, 0])
+        nc.vector.tensor_copy(out=xt_sw[64:128, :].bitcast(I32), in_=xt_s[64:128, T : 2 * T].bitcast(I32))
+        nc.vector.tensor_copy(out=xt_sw[0:64, :].bitcast(I32), in_=xt_s[64:128, 0:T].bitcast(I32))
         H = J // 2
         for u in range(2):
             cols, lcols = slice(H * u, H * (u + 1)), slice(H // 16 * u, H // 16 * (u + 1))
@@ -113,6 +113,11 @@ def tile_list_groupboard_crossed_one_plain_kernel(
         w2_dealt = w2_raw[:].rearrange("p (m t) -> p t m", t=PACK)
         for t in range(PACK):
             nc.scalar.copy(out=w2_p[t][:], in_=w2_dealt[:, t])
+
+        for t, tag in ((2, "ws_raw"), (3, "w_raw")):
+            page = keep.tile([P, C], F32, name=f"page{t}", tag=tag, align_bytes=64)
+            nc.gpsimd.memset(page[:], 0.0)
+            pages.append(page)
 
         b_pick = keep.tile([P, PACK, O], F32, name="b_pick")
         diff = keep.tile([P, PACK, O], F32, name="diff")

from contextlib import ExitStack

import concourse.mybir as mybir

F32 = mybir.dt.float32
BF16 = mybir.dt.bfloat16
I32 = mybir.dt.int32
U32 = mybir.dt.uint32
U16 = mybir.dt.uint16
U8 = mybir.dt.uint8
E4M3 = mybir.dt.float8_e4m3fn_x4
E5M2 = mybir.dt.float8_e5m2_x4
E2M1 = mybir.dt.float4_e2m1fn_x4
ACT = mybir.ActivationFunctionType
ALU = mybir.AluOpType

P = 128
PACK = 4
K, T, Z, J, R, C, O, N = 512, 1024, 1024, 256, 512, 512, 128, 256

FLOPS = 4 * 2 * K * R * J + 2 * R * N * O


def load_plane(queue, plane, scales):
    rows = scales[0].bitcast(I32)
    for r in range(4):
        queue.dma_start(out=plane[r:P:32, :].bitcast(I32), in_=rows[r:16:4, :])


def tile_list_groupboard_crossed_one_plain_kernel(
    tc, xt_words, xt_scales, xo_words, xo_scales, w_words, w_scales, w2_words, w2_scales,
    sa, wb_words, wb_scales, offs, offs2, offs3, offs4, offs5, out,
):
    nc = tc.nc
    with ExitStack() as ctx:
        keep = ctx.enter_context(tc.tile_pool(name="keep", bufs=1))
        psum = ctx.enter_context(tc.psum_pool(name="psum", bufs=1))

        list1 = keep.tile([P, J // 16], U16, name="list1")
        list2 = keep.tile([P, J // 16], U16, name="list2")
        list3 = keep.tile([P, J // 16], U16, name="list3")
        list4 = keep.tile([P, O // 16], U16, name="list4")
        list5 = keep.tile([P, O // 16], U16, name="list5")

        xt_w = keep.tile([P, T], U16, name="xt_w", align_bytes=64)
        xo_w = keep.tile([P, Z], U32, name="xo_w", align_bytes=64)
        xt_s = keep.tile([P, 2 * T], U8, name="xt_s", align_bytes=64)
        xo_s = keep.tile([P, Z], U8, name="xo_s", align_bytes=64)
        ws_raw = keep.tile([4, 8 * R], U8, name="ws_raw", tag="ws_raw", align_bytes=64)
        ws_pl = keep.tile([P, 2 * R], U8, name="ws_pl", align_bytes=64)
        w_raw = keep.tile([P, R], U32, name="w_raw", tag="w_raw", align_bytes=64)
        w2_raw = keep.tile([P, R], U32, name="w2_raw", align_bytes=64)
        wb_w = keep.tile([P, 2 * N], U8, name="wb_w", align_bytes=64)
        wb_s = keep.tile([P, N], U8, name="wb_s", align_bytes=64)
        sa_t = keep.tile([P, PACK], F32, name="sa_t")
        pages = [keep.tile([P, C], F32, name=f"page{t}") for t in range(2)]

        nc.vector.memset(xt_s[64:128, :].bitcast(I32), 0)
        nc.vector.memset(xo_s[:].bitcast(I32), 0)
        nc.vector.memset(wb_s[:].bitcast(I32), 0)
        nc.vector.memset(ws_pl[:].bitcast(I32), 0)
        for t in range(2):
            nc.vector.memset(pages[t][:], 0.0)

        nc.sync.dma_start(out=xt_w[:].bitcast(I32), in_=xt_words[0].bitcast(I32))
        ws_blocks = ws_raw[:].bitcast(I32).rearrange("p (q a c) -> p a q c", q=4, a=2)
        xt_rows = xt_scales[0].bitcast(I32).rearrange("(h q r) c -> q r h c", h=2, q=2)
        for a, scales in enumerate((w2_scales, w_scales)):
            p0 = 64 + 32 * a
            nc.sync.dma_start(out=ws_blocks[:, a], in_=scales[0].bitcast(I32).rearrange("(q r) c -> r q c", q=4))
            nc.sync.dma_start(out=xt_s[p0 : p0 + 4, :].bitcast(I32).rearrange("p (h c) -> p h c", h=2), in_=xt_rows[a])
        nc.sync.dma_start(list1[:], offs)
        nc.sync.dma_start(out=xo_w[:].bitcast(I32), in_=xo_words[0].rearrange("p n t -> p (n t)").bitcast(I32))
        nc.sync.dma_start(out=w_raw[:].bitcast(I32), in_=w_words[0].rearrange("p n t -> p (n t)").bitcast(I32))
        nc.sync.dma_start(list2[:], offs2)
        nc.sync.dma_start(out=w2_raw[:].bitcast(I32), in_=w2_words[0].rearrange("p n t -> p (n t)").bitcast(I32))
        load_plane(nc.sync, xo_s, xo_scales)
        nc.sync.dma_start(list3[:], offs3)
        nc.sync.dma_start(list5[:], offs5)
        nc.sync.dma_start(list4[:], offs4)

        nc.sync.dma_start(out=sa_t[:], in_=sa.rearrange("(p t) o -> p (t o)", t=PACK))
        nc.sync.dma_start(out=wb_w[:].bitcast(I32), in_=wb_words[0].bitcast(I32))
        load_plane(nc.sync, wb_s, wb_scales)

        xt_g = keep.tile([P, J], U16, name="xt_g", align_bytes=64)
        xo_g = keep.tile([P, J], U32, name="xo_g", align_bytes=64)
        xt_gs = keep.tile([P, J], U8, name="xt_gs", align_bytes=64)
        xo_gs = keep.tile([P, J], U8, name="xo_gs", align_bytes=64)
        ws = [keep.tile([P, 2, P], U8, name=f"ws{t}", align_bytes=64) for t in range(PACK)]
        w_p = keep.tile([P, PACK, P], U32, name="w_p", align_bytes=64)
        w2_p = [keep.tile([P, P], U32, name=f"w2_p{t}", align_bytes=64) for t in range(PACK)]

        xt_sw = keep.tile([P, T], U8, name="xt_sw", align_bytes=64)
        for q in range(4):
            nc.vector.tensor_copy(out=ws_pl[32 * q : 32 * q + 4, :].bitcast(I32),
                                  in_=ws_raw[0:4, 2 * R * q : 2 * R * (q + 1)].bitcast(I32))
        ws_dealt = ws_pl[:].rearrange("p (a m t) -> p t a m", a=2, t=PACK)
        nc.vector.tensor_copy(out=ws[0][:], in_=ws_dealt[:, 0])
        nc.vector.tensor_copy(out=xt_sw[64:128, :].bitcast(I32), in_=xt_s[64:128, T : 2 * T].bitcast(I32))
        nc.vector.tensor_copy(out=xt_sw[0:64, :].bitcast(I32), in_=xt_s[64:128, 0:T].bitcast(I32))
        H = J // 2
        for u in range(2):
            cols, lcols = slice(H * u, H * (u + 1)), slice(H // 16 * u, H // 16 * (u + 1))
            nc.vector.tensor_copy(xt_gs[:, cols], xt_sw[:].indirect(list1[:, lcols]))
            nc.vector.tensor_copy(xt_g[:, cols], xt_w[:].indirect(list1[:, lcols]))
            nc.vector.tensor_copy(xo_g[:, cols], xo_w[:].indirect(list2[:, lcols]))
            nc.vector.tensor_copy(xo_gs[:, cols], xo_s[:].indirect(list2[:, lcols]))
        for t in range(1, PACK):
            nc.gpsimd.tensor_copy(out=ws[t][:], in_=ws_dealt[:, t])

        nc.scalar.copy(out=w_p[:].rearrange("p t m -> p m t"), in_=w_raw[:].rearrange("p (m t) -> p m t", t=PACK))
        w2_dealt = w2_raw[:].rearrange("p (m t) -> p t m", t=PACK)
        for t in range(PACK):
            nc.scalar.copy(out=w2_p[t][:], in_=w2_dealt[:, t])

        for t, tag in ((2, "ws_raw"), (3, "w_raw")):
            page = keep.tile([P, C], F32, name=f"page{t}", tag=tag, align_bytes=64)
            nc.gpsimd.memset(page[:], 0.0)
            pages.append(page)

        b_pick = keep.tile([P, PACK, O], F32, name="b_pick")
        diff = keep.tile([P, PACK, O], F32, name="diff")
        a_sb = [keep.tile([P, J], F32, name=f"a_sb{t}") for t in range(PACK)]
        b_sb = [keep.tile([P, J], F32, name=f"b_sb{t}", tag=f"b_sb{t}") for t in range(PACK)]

        def product(acc, first, second):
            for n, (lhs, rhs) in enumerate((first, second)):
                nc.tensor.matmul_mx(acc, lhsT=lhs[0], lhsT_scale=lhs[1], rhs=rhs[0], rhs_scale=rhs[1],
                                    start=(n == 0), stop=(n == 1))

        def tokens(cols):
            return xt_g[:, cols].bitcast(E2M1), xt_gs[:, cols]

        def notes(cols):
            return xo_g[:, cols].bitcast(E4M3), xo_gs[:, cols]

        first = [(w_p[:, t, :].bitcast(E4M3), ws[t][:, 1, :]) for t in range(PACK)]
        second = [(w2_p[t][:].bitcast(E5M2), ws[t][:, 0, :]) for t in range(PACK)]
        whole = slice(0, J)
        for u in range(2):
            cols, lcols = slice(H * u, H * (u + 1)), slice(H // 16 * u, H // 16 * (u + 1))
            a_half = psum.tile([P, H], F32, name="a_half", tag=("a0", "b3")[u])
            product(a_half[:], (first[0], tokens(cols)), (second[0], notes(cols)))
            nc.scalar.copy(out=a_sb[0][:, cols], in_=a_half[:])
            nc.vector.tensor_copy(pages[0][:].indirect(list3[:, lcols]), a_sb[0][:, cols])
        for t in range(1, PACK):
            a_ps = psum.tile([P, J], F32, name="a_ps", tag=f"a{t}")
            product(a_ps[:], (second[t], notes(whole)), (first[t], tokens(whole)))
            nc.scalar.copy(out=a_sb[t][:], in_=a_ps[:])
            nc.vector.tensor_copy(pages[t][:].indirect(list3[:]), a_sb[t][:])
        for t in range(PACK):
            b_ps = psum.tile([P, J], F32, name="b_ps", tag=f"b{t}")
            product(b_ps[:], (first[t], notes(whole)), (second[t], tokens(whole)))
            nc.scalar.copy(out=b_sb[t][:], in_=b_ps[:])
            nc.scalar.activation(b_pick[:, t, :], b_sb[t][:].indirect(list5[:]), ACT.Copy)
        picked = [keep.tile([P, 2, O], F32, name=f"picked{u}", tag=f"b_sb{2 + u}") for u in range(2)]
        for t in range(PACK):
            nc.scalar.activation(picked[t // 2][:, t % 2, :], pages[t][:].indirect(list4[:]), ACT.Copy, scale=sa_t[:, t : t + 1])

        nc.vector.tensor_tensor(diff[:, 0:2, :], picked[0][:], b_pick[:, 0:2, :], ALU.subtract)
        for t in (2, 3):
            nc.vector.tensor_tensor(diff[:, t, :], picked[1][:, t - 2, :], b_pick[:, t, :], ALU.subtract)
        hid = keep.tile([P, O, PACK], BF16, name="hid", align_bytes=64)
        for u in range(2):
            nc.scalar.activation(hid[:, :, 2 * u : 2 * u + 2],
                                 diff[:, 2 * u : 2 * u + 2, :].rearrange("p t o -> p o t"), ACT.Abs)
        hid_w = keep.tile([P, O], U32, name="hid_w", align_bytes=64)
        hid_s = keep.tile([P, O], U8, name="hid_s", align_bytes=64)
        nc.vector.quantize_mx(out=hid_w[:].bitcast(E5M2), scales=hid_s[:], in_=hid[:].rearrange("p o t -> p (o t)"))

        for h in range(2):
            y_ps = psum.tile([P, O], F32, name="y_ps", tag=f"a{h}")
            nc.tensor.matmul_mx(y_ps[:], lhsT=wb_w[:, 2 * P * h : 2 * P * (h + 1)].bitcast(E2M1),
                                lhsT_scale=wb_s[:, P * h : P * (h + 1)],
                                rhs=hid_w[:].bitcast(E5M2), rhs_scale=hid_s[:], start=True, stop=True)
            y_sb = keep.tile([P, O], F32, name=f"y_sb{h}")
            if h == 0:
                nc.vector.tensor_copy(out=y_sb[:], in_=y_ps[:])
                nc.sync.dma_start(out=out[0:P, :], in_=y_sb[:])
            else:
                nc.scalar.copy(out=y_sb[:], in_=y_ps[:])
                nc.scalar.dma_start(out=out[P : 2 * P, :], in_=y_sb[:])
